import numpy as np
import ml_dtypes


def mxq(x, axis, fmt="e4m3"):
    dtype, down = {"e4m3": (ml_dtypes.float8_e4m3fn, 7), "e5m2": (ml_dtypes.float8_e5m2, 14)}[fmt]
    v = np.moveaxis(np.asarray(x, np.float32).astype(ml_dtypes.bfloat16).astype(np.float64), axis, -1)
    blocks = v.reshape(v.shape[:-1] + (-1, 32))
    amax = np.abs(blocks).max(-1, keepdims=True)
    byte = np.maximum(np.where(amax > 0, np.frexp(amax)[1] - 1 + 127, 0) - down, 1)
    scale = np.exp2(byte - 127.0)
    codes = (blocks / scale).astype(np.float32).astype(dtype).astype(np.float64)
    return np.moveaxis((codes * scale).reshape(v.shape), -1, axis)


WIDE = False


def mx_kscale(k):
    if not WIDE:
        return np.ones(k)
    levels = np.array([10, -10, 5, -5, 0])
    if k % 512:
        return np.exp2(np.random.permutation(np.resize(levels, k // 32))).repeat(32)
    a = np.empty((k // 512, 16))
    for p in range(k // 512):
        a[p, :8] = np.random.permutation(np.resize(levels, 8))
        for g in range(8):
            far = levels[np.abs(levels - a[p, g]) >= 10]
            a[p, g + 8] = far[np.random.randint(len(far))]
    return np.exp2(a.ravel()).repeat(32)


def f64(x):
    return np.asarray(x).astype(np.float64)


def striped(idx):
    return np.tile(np.asarray(idx).reshape(-1, 16).T, (8, 1)).astype(np.uint16)


def unstriped(offs):
    return offs[:16].T.reshape(-1).astype(np.int64)


E2M1 = np.array([0.0, 0.5, 1.0, 1.5, 2.0, 3.0, 4.0, 6.0, -0.0, -0.5, -1.0, -1.5, -2.0, -3.0, -4.0, -6.0])


def pack_weight(w, fmt):
    k, n = w.shape
    w = f64(np.asarray(w, np.float32).astype(ml_dtypes.bfloat16)).reshape(k // 32, 32, n)
    amax = np.abs(w).max(1)
    if fmt == "e4m3":
        byte = np.frexp(amax)[1] - 1 + 127 - 7
    else:
        mant, ex = np.frexp(amax / 6.0)
        byte = np.where(mant > 0.5, ex, ex - 1) + 127
    byte = np.clip(np.where(amax > 0, byte, 1), 1, 254)
    scaled = (w * np.exp2(127.0 - byte)[:, None, :]).reshape(k, n).astype(np.float32)
    by_word = np.ascontiguousarray(scaled.reshape(k // 512, 128, 4, n).transpose(0, 1, 3, 2))
    if fmt == "e4m3":
        words = by_word.astype(ml_dtypes.float8_e4m3fn).view(np.uint8)
    else:
        c = by_word.astype(ml_dtypes.float4_e2m1fn).view(np.uint8) & 0xF
        words = (c[..., 0::2] | (c[..., 1::2] << 4)).reshape(k // 512, 128, 2 * n)
    return np.ascontiguousarray(words), np.ascontiguousarray(byte.astype(np.uint8).reshape(k // 512, 16, n))


def unpack_weight(words, scales, fmt):
    g, _, n = scales.shape
    words = np.ascontiguousarray(words).reshape(g, 128, n, -1)
    if fmt == "e4m3":
        vals = words.view(ml_dtypes.float8_e4m3fn).astype(np.float64)
    else:
        nib = np.empty((g, 128, n, 4), np.uint8)
        nib[..., 0::2] = words & 0xF
        nib[..., 1::2] = words >> 4
        vals = E2M1[nib]
    vals = vals * np.repeat(np.exp2(scales.astype(np.float64) - 127.0), 8, axis=1)[..., None]
    return vals.transpose(0, 1, 3, 2).reshape(g * 512, n)


K, T, R, J, M = 512, 512, 2048, 512, 512


def setup_inputs():
    n = np.random.standard_normal
    idx = np.random.permutation(R)[:J]
    fk = mx_kscale(K)
    fj = mx_kscale(J)
    tj = np.ones(R)
    tj[idx] = fj
    xtp = pack_weight(n((K, T)) / fk[:, None], "e4m3")
    wyp = pack_weight(n((K, M)) * 1 / np.sqrt(K) * fk[:, None], "e2m1")
    return {
        "xt_words": xtp[0],
        "xt_scales": xtp[1],
        "wu": (n((K, R)) * 1 / np.sqrt(K) * fk[:, None] * tj).astype(np.float32),
        "wd": (n((M, R)) * (1 / np.sqrt(J)) / tj).astype(np.float32),
        "wy_words": wyp[0],
        "wy_scales": wyp[1],
        "offs": striped(idx),
    }


def reference(xt_words, xt_scales, wu, wd, wy_words, wy_scales, offs):
    idx = unstriped(offs)
    xtu = unpack_weight(xt_words, xt_scales, "e4m3")
    wyu = unpack_weight(wy_words, wy_scales, "e2m1")
    wuidxq = mxq(f64(wu)[:, idx], 0, "e4m3")
    a = wuidxq.T @ xtu
    hid = np.maximum(a, 0.0)
    dj = f64(wd)[:, idx].T
    djq = mxq(dj, 0, "e4m3")
    hidq = mxq(hid, 0, "e4m3")
    y = djq.T @ hidq + wyu.T @ xtu
    return y

@@ -1,0 +1,129 @@
+from contextlib import ExitStack
+
+import concourse.mybir as mybir
+from concourse.masks import make_identity
+
+K, T, R, J, M = 512, 512, 2048, 512, 512
+FLOPS = 2 * T * (K * J + J * M + K * M)
+
+F32 = mybir.dt.float32
+BF16 = mybir.dt.bfloat16
+I32 = mybir.dt.int32
+U32 = mybir.dt.uint32
+U16 = mybir.dt.uint16
+U8 = mybir.dt.uint8
+FP8X4 = mybir.dt.float8_e4m3fn_x4
+FP4X4 = mybir.dt.float4_e2m1fn_x4
+RELU = mybir.ActivationFunctionType.Relu
+
+P = 128
+PACK = 4
+CHUNKS = M // P
+
+
+def tile_list_hot_neurons_kernel(tc, xt_words, xt_scales, wu, wd, wy_words, wy_scales, offs, out):
+    nc = tc.nc
+    with ExitStack() as ctx:
+        keep = ctx.enter_context(tc.tile_pool(name="keep", bufs=1))
+        psum = ctx.enter_context(tc.psum_pool(name="psum", bufs=1))
+
+        offsets = keep.tile([P, J // 16], U16, name="offsets")
+        wu_rows = [keep.tile([P, R], F32, name="wu%d" % i) for i in range(PACK)]
+        wd_rows = [keep.tile([P, R], F32, name="wd%d" % c, tag="wd%d" % c, align_bytes=64) for c in range(CHUNKS)]
+        x_codes = keep.tile([P, T], I32, name="x_codes", align_bytes=64)
+        y_codes = keep.tile([P, 2 * M], U8, name="y_codes", align_bytes=64)
+        x_plane = keep.tile([P, T], U8, name="x_plane", align_bytes=64)
+        y_plane = keep.tile([P, M], U8, name="y_plane", align_bytes=64)
+        ident = keep.tile([P, P], F32, name="ident")
+
+        def load_plane(plane, scales):
+            for q in range(4):
+                nc.sync.dma_start(out=plane[32 * q:32 * q + 4, :].bitcast(I32),
+                                  in_=scales[0, 4 * q:4 * q + 4, :].bitcast(I32))
+
+        nc.gpsimd.memset(x_plane[:].bitcast(I32), 0)
+        nc.gpsimd.memset(y_plane[:].bitcast(I32), 0)
+        make_identity(nc, ident[:])
+        wu_by_slot = wu.rearrange("(p i) r -> i p r", i=PACK)
+        nc.sync.dma_start(out=wu_rows[0][:], in_=wu_by_slot[0])
+        nc.sync.dma_start(offsets[:], offs)
+        load_plane(x_plane, xt_scales)
+        for i in range(1, PACK):
+            nc.sync.dma_start(out=wu_rows[i][:], in_=wu_by_slot[i])
+        nc.sync.dma_start(out=x_codes[:], in_=xt_words[0].rearrange("p n t -> p (n t)").bitcast(I32))
+        load_plane(y_plane, wy_scales)
+        nc.sync.dma_start(out=y_codes[:].bitcast(I32), in_=wy_words[0].bitcast(I32))
+        for c in range(CHUNKS):
+            nc.sync.dma_start(out=wd_rows[c][:], in_=wd[c * P:(c + 1) * P, :])
+
+        wu_bf = keep.tile([P, PACK * J], BF16, name="wu_bf", tag="before_pick0", align_bytes=64)
+        wu_view = wu_bf[:].rearrange("p (u e g r i) -> p i g u r e", u=2, e=2, g=16, r=8, i=PACK)
+        for i in range(PACK):
+            nc.vector.tensor_copy(out=wu_view[:, i], in_=wu_rows[i][:].indirect(offsets[:]))
+        u_codes = keep.tile([P, J], U32, name="u_codes", align_bytes=64)
+        u_plane = keep.tile([P, J], U8, name="u_plane", align_bytes=64)
+        nc.vector.quantize_mx(out=u_codes[:].bitcast(FP8X4), scales=u_plane[:], in_=wu_bf[:])
+
+        h_codes = keep.tile([P, T], U32, name="h_codes", tag="wd1", align_bytes=64)
+        h_plane = keep.tile([P, T], U8, name="h_plane", align_bytes=64)
+        h_bf = keep.tile([P, PACK * T], BF16, name="h_bf", tag="h_bf", align_bytes=64)
+        for b in range(4):
+            toks = slice(b * P, (b + 1) * P)
+            acc = psum.tile([P, PACK, P], F32, name="acc%d" % b, tag="acc%d" % b)
+            for s in range(PACK):
+                cols = slice(s * P, (s + 1) * P)
+                nc.tensor.matmul_mx(out=acc[:, s, :], lhsT=u_codes[:, cols].bitcast(FP8X4), lhsT_scale=u_plane[:, cols],
+                                    rhs=x_codes[:, toks].bitcast(FP8X4), rhs_scale=x_plane[:, toks],
+                                    start=True, stop=True)
+            dst = h_bf[:, b * PACK * P:(b + 1) * PACK * P].rearrange("p (t s) -> p t s", s=PACK)
+            nc.scalar.activation(out=dst, in_=acc[:].rearrange("p s t -> p t s"), func=RELU)
+        nc.vector.quantize_mx(out=h_codes[:].bitcast(FP8X4), scales=h_plane[:], in_=h_bf[:])
+
+        for c in range(CHUNKS):
+            picked = keep.tile([P, J], BF16, name="picked%d" % c, tag="before_pick%d" % c, align_bytes=64)
+            nc.vector.tensor_copy(out=picked[:].rearrange("p (u g i) -> p g u i", u=2, g=16),
+                                  in_=wd_rows[c][:].indirect(offsets[:]))
+            words = picked[:].bitcast(F32)
+            turned = psum.tile([P, 2, P], F32, name="turned%d" % c, tag="turned%d" % (c % 2))
+            for u in range(2):
+                nc.tensor.transpose(turned[:, u, :], words[:, u * P:(u + 1) * P], ident[:])
+            d_bf = keep.tile([P, PACK * P], BF16, name="d_bf%d" % c,
+                             tag=("d_bf0", "before_pick2", "before_pick3", "d_bf3")[c], align_bytes=64)
+            nc.scalar.copy(out=d_bf[:].bitcast(F32).rearrange("p (m u) -> p m u", u=2),
+                           in_=turned[:].rearrange("p u m -> p m u"))
+            d_codes = keep.tile([P, P], U32, name="d_codes%d" % c, tag=("h_bf", "d_codes1", "d_codes2", "d_codes3")[c],
+                                align_bytes=64)
+            d_plane = keep.tile([P, P], U8, name="d_plane%d" % c, align_bytes=64)
+            nc.vector.quantize_mx(out=d_codes[:].bitcast(FP8X4), scales=d_plane[:], in_=d_bf[:])
+
+            y_w = y_codes[:, 2 * c * P:2 * (c + 1) * P].bitcast(FP4X4)
+            y_s = y_plane[:, c * P:(c + 1) * P]
+            res = keep.tile([P, T], F32, name="res%d" % c)
+            rows = slice(c * P, (c + 1) * P)
+            if c < CHUNKS - 1:
+                acc = psum.tile([P, T], F32, name="total%d" % c, tag=("total0", "total1", "acc0")[c])
+                nc.tensor.matmul_mx(out=acc[:], lhsT=y_w, lhsT_scale=y_s,
+                                    rhs=x_codes[:].bitcast(FP8X4), rhs_scale=x_plane[:], start=True, stop=False)
+                nc.tensor.matmul_mx(out=acc[:], lhsT=d_codes[:].bitcast(FP8X4), lhsT_scale=d_plane[:],
+                                    rhs=h_codes[:].bitcast(FP8X4), rhs_scale=h_plane[:], start=False, stop=True)
+                nc.scalar.copy(out=res[:], in_=acc[:])
+                nc.sync.dma_start(out=out[rows, :], in_=res[:])
+            else:
+                accs = [psum.tile([P, P], F32, name="last%d" % b, tag=("acc1", "acc2", "acc3", "total0")[b])
+                        for b in range(4)]
+                for b in range(4):
+                    toks = slice(b * P, (b + 1) * P)
+                    nc.tensor.matmul_mx(out=accs[b][:], lhsT=y_w, lhsT_scale=y_s,
+                                        rhs=x_codes[:, toks].bitcast(FP8X4), rhs_scale=x_plane[:, toks],
+                                        start=True, stop=False)
+                for b in range(4):
+                    toks = slice(b * P, (b + 1) * P)
+                    nc.tensor.matmul_mx(out=accs[b][:], lhsT=d_codes[:].bitcast(FP8X4), lhsT_scale=d_plane[:],
+                                        rhs=h_codes[:, toks].bitcast(FP8X4), rhs_scale=h_plane[:, toks],
+                                        start=False, stop=True)
+                    if b % 2 == 0:
+                        nc.vector.tensor_copy(out=res[:, toks], in_=accs[b][:])
+                    else:
+                        nc.scalar.copy(out=res[:, toks], in_=accs[b][:])
+                        half = slice((b - 1) * P, (b + 1) * P)
+                        nc.sync.dma_start(out=out[rows, half], in_=res[:, half])

@@ -25,11 +25,12 @@ def tile_list_hot_neurons_kernel(tc, xt_words, xt_scales, wu, wd, wy_words, wy_s
     nc = tc.nc
     with ExitStack() as ctx:
         keep = ctx.enter_context(tc.tile_pool(name="keep", bufs=1))
+        placed = ctx.enter_context(tc.tile_pool(name="placed", bufs=1))
         psum = ctx.enter_context(tc.psum_pool(name="psum", bufs=1))
 
         offsets = keep.tile([P, J // 16], U16, name="offsets")
         wu_rows = [keep.tile([P, R], F32, name="wu%d" % i) for i in range(PACK)]
-        wd_rows = [keep.tile([P, R], F32, name="wd%d" % c, tag="wd%d" % c, align_bytes=64) for c in range(CHUNKS)]
+        wd_rows = [placed.tile([P, R], F32, name="wd%d" % c, offset=c * 4 * R, align_bytes=64) for c in range(CHUNKS)]
         x_codes = keep.tile([P, T], I32, name="x_codes", align_bytes=64)
         y_codes = keep.tile([P, 2 * M], U8, name="y_codes", align_bytes=64)
         x_plane = keep.tile([P, T], U8, name="x_plane", align_bytes=64)
@@ -56,7 +57,7 @@ def tile_list_hot_neurons_kernel(tc, xt_words, xt_scales, wu, wd, wy_words, wy_s
         for c in range(CHUNKS):
             nc.sync.dma_start(out=wd_rows[c][:], in_=wd[c * P:(c + 1) * P, :])
 
-        wu_bf = keep.tile([P, PACK * J], BF16, name="wu_bf", tag="before_pick0", align_bytes=64)
+        wu_bf = keep.tile([P, PACK * J], BF16, name="wu_bf", tag="wu_bf", align_bytes=64)
         wu_view = wu_bf[:].rearrange("p (u e g r i) -> p i g u r e", u=2, e=2, g=16, r=8, i=PACK)
         for i in range(PACK):
             nc.vector.tensor_copy(out=wu_view[:, i], in_=wu_rows[i][:].indirect(offsets[:]))
@@ -64,9 +65,10 @@ def tile_list_hot_neurons_kernel(tc, xt_words, xt_scales, wu, wd, wy_words, wy_s
         u_plane = keep.tile([P, J], U8, name="u_plane", align_bytes=64)
         nc.vector.quantize_mx(out=u_codes[:].bitcast(FP8X4), scales=u_plane[:], in_=wu_bf[:])
 
-        h_codes = keep.tile([P, T], U32, name="h_codes", tag="wd1", align_bytes=64)
-        h_plane = keep.tile([P, T], U8, name="h_plane", align_bytes=64)
-        h_bf = keep.tile([P, PACK * T], BF16, name="h_bf", tag="h_bf", align_bytes=64)
+        h_codes = [placed.tile([P, T // 2], U32, name="h_codes%d" % h, offset=h * 4 * R, align_bytes=64) for h in range(2)]
+        h_plane = [keep.tile([P, T // 2], U8, name="h_plane%d" % h, align_bytes=64) for h in range(2)]
+        h_bf = [keep.tile([P, PACK * T // 2], BF16, name="h_bf%d" % h, tag="h_bf%d" % h, align_bytes=64)
+                for h in range(2)]
         for b in range(4):
             toks = slice(b * P, (b + 1) * P)
             acc = psum.tile([P, PACK, P], F32, name="acc%d" % b, tag="acc%d" % b)
@@ -75,24 +77,27 @@ def tile_list_hot_neurons_kernel(tc, xt_words, xt_scales, wu, wd, wy_words, wy_s
                 nc.tensor.matmul_mx(out=acc[:, s, :], lhsT=u_codes[:, cols].bitcast(FP8X4), lhsT_scale=u_plane[:, cols],
                                     rhs=x_codes[:, toks].bitcast(FP8X4), rhs_scale=x_plane[:, toks],
                                     start=True, stop=True)
-            dst = h_bf[:, b * PACK * P:(b + 1) * PACK * P].rearrange("p (t s) -> p t s", s=PACK)
+            dst = h_bf[b // 2][:, (b % 2) * PACK * P:(b % 2 + 1) * PACK * P].rearrange("p (t s) -> p t s", s=PACK)
             nc.scalar.activation(out=dst, in_=acc[:].rearrange("p s t -> p t s"), func=RELU)
-        nc.vector.quantize_mx(out=h_codes[:].bitcast(FP8X4), scales=h_plane[:], in_=h_bf[:])
+            if b % 2 == 1:
+                nc.vector.quantize_mx(out=h_codes[b // 2][:].bitcast(FP8X4), scales=h_plane[b // 2][:], in_=h_bf[b // 2][:])
 
         for c in range(CHUNKS):
-            picked = keep.tile([P, J], BF16, name="picked%d" % c, tag="before_pick%d" % c, align_bytes=64)
+            picked = keep.tile([P, J], BF16, name="picked%d" % c, align_bytes=64)
             nc.vector.tensor_copy(out=picked[:].rearrange("p (u g i) -> p g u i", u=2, g=16),
                                   in_=wd_rows[c][:].indirect(offsets[:]))
             words = picked[:].bitcast(F32)
-            turned = psum.tile([P, 2, P], F32, name="turned%d" % c, tag="turned%d" % (c % 2))
+            turned = psum.tile([P, 2, P], F32, name="turned%d" % c, tag=("acc0", "acc3", "turned2", "turned3")[c])
             for u in range(2):
                 nc.tensor.transpose(turned[:, u, :], words[:, u * P:(u + 1) * P], ident[:])
             d_bf = keep.tile([P, PACK * P], BF16, name="d_bf%d" % c,
-                             tag=("d_bf0", "before_pick2", "before_pick3", "d_bf3")[c], align_bytes=64)
+                             tag="d_bf%d" % c, align_bytes=64)
             nc.scalar.copy(out=d_bf[:].bitcast(F32).rearrange("p (m u) -> p m u", u=2),
                            in_=turned[:].rearrange("p u m -> p m u"))
-            d_codes = keep.tile([P, P], U32, name="d_codes%d" % c, tag=("h_bf", "d_codes1", "d_codes2", "d_codes3")[c],
-                                align_bytes=64)
+            if c < CHUNKS - 1:
+                d_codes = placed.tile([P, P], U32, name="d_codes%d" % c, offset=(c + 1) * 4 * R + 2 * T, align_bytes=64)
+            else:
+                d_codes = keep.tile([P, P], U32, name="d_codes%d" % c, align_bytes=64)
             d_plane = keep.tile([P, P], U8, name="d_plane%d" % c, align_bytes=64)
             nc.vector.quantize_mx(out=d_codes[:].bitcast(FP8X4), scales=d_plane[:], in_=d_bf[:])
 
@@ -101,29 +106,34 @@ def tile_list_hot_neurons_kernel(tc, xt_words, xt_scales, wu, wd, wy_words, wy_s
             res = keep.tile([P, T], F32, name="res%d" % c)
             rows = slice(c * P, (c + 1) * P)
             if c < CHUNKS - 1:
-                acc = psum.tile([P, T], F32, name="total%d" % c, tag=("total0", "total1", "acc0")[c])
+                acc = psum.tile([P, T], F32, name="total%d" % c, tag=("acc0", "acc3", "turned2")[c])
+                if c == CHUNKS - 2:
+                    nc.tensor.matmul_mx(out=acc[:], lhsT=y_w, lhsT_scale=y_s,
+                                        rhs=x_codes[:].bitcast(FP8X4), rhs_scale=x_plane[:], start=True, stop=True)
                 nc.tensor.matmul_mx(out=acc[:], lhsT=y_w, lhsT_scale=y_s,
                                     rhs=x_codes[:].bitcast(FP8X4), rhs_scale=x_plane[:], start=True, stop=False)
-                nc.tensor.matmul_mx(out=acc[:], lhsT=d_codes[:].bitcast(FP8X4), lhsT_scale=d_plane[:],
-                                    rhs=h_codes[:].bitcast(FP8X4), rhs_scale=h_plane[:], start=False, stop=True)
+                for h in range(2):
+                    nc.tensor.matmul_mx(out=acc[:, h * (T // 2):(h + 1) * (T // 2)],
+                                        lhsT=d_codes[:].bitcast(FP8X4), lhsT_scale=d_plane[:],
+                                        rhs=h_codes[h][:].bitcast(FP8X4), rhs_scale=h_plane[h][:],
+                                        start=False, stop=(h == 1))
                 nc.scalar.copy(out=res[:], in_=acc[:])
                 nc.sync.dma_start(out=out[rows, :], in_=res[:])
             else:
-                accs = [psum.tile([P, P], F32, name="last%d" % b, tag=("acc1", "acc2", "acc3", "total0")[b])
-                        for b in range(4)]
+                accs = [psum.tile([P, T // 2], F32, name="last%d" % h, tag=("acc0", "acc3")[h]) for h in range(2)]
                 for b in range(4):
                     toks = slice(b * P, (b + 1) * P)
-                    nc.tensor.matmul_mx(out=accs[b][:], lhsT=y_w, lhsT_scale=y_s,
+                    part = slice((b % 2) * P, (b % 2 + 1) * P)
+                    nc.tensor.matmul_mx(out=accs[b // 2][:, part], lhsT=y_w, lhsT_scale=y_s,
                                         rhs=x_codes[:, toks].bitcast(FP8X4), rhs_scale=x_plane[:, toks],
-                                        start=True, stop=False)
-                for b in range(4):
-                    toks = slice(b * P, (b + 1) * P)
-                    nc.tensor.matmul_mx(out=accs[b][:], lhsT=d_codes[:].bitcast(FP8X4), lhsT_scale=d_plane[:],
-                                        rhs=h_codes[:, toks].bitcast(FP8X4), rhs_scale=h_plane[:, toks],
+                                        start=(b % 2 == 0), stop=False)
+                for h in range(2):
+                    half = slice(h * (T // 2), (h + 1) * (T // 2))
+                    nc.tensor.matmul_mx(out=accs[h][:], lhsT=d_codes[:].bitcast(FP8X4), lhsT_scale=d_plane[:],
+                                        rhs=h_codes[h][:].bitcast(FP8X4), rhs_scale=h_plane[h][:],
                                         start=False, stop=True)
-                    if b % 2 == 0:
-                        nc.vector.tensor_copy(out=res[:, toks], in_=accs[b][:])
+                    if h == 0:
+                        nc.vector.tensor_copy(out=res[:, half], in_=accs[h][:])
                     else:
-                        nc.scalar.copy(out=res[:, toks], in_=accs[b][:])
-                        half = slice((b - 1) * P, (b + 1) * P)
-                        nc.sync.dma_start(out=out[rows, half], in_=res[:, half])
+                        nc.scalar.copy(out=res[:, half], in_=accs[h][:])
+                    nc.sync.dma_start(out=out[rows, half], in_=res[:, half])

@@ -18,7 +18,17 @@ RELU = mybir.ActivationFunctionType.Relu
 
 P = 128
 PACK = 4
+BLOCKS = J // 32
+QUADRANTS = 4
 CHUNKS = M // P
+LAST = CHUNKS - 1
+QUARTERS = T // P
+HALF = T // 2
+ROW_BYTES = 4 * R
+CODE_BYTES = 4 * P
+
+TURN_BANK = ("acc0", "acc3", "turn2", "turn3")
+LAST_BANK = ("acc1", "acc2")
 
 
 def tile_list_hot_neurons_kernel(tc, xt_words, xt_scales, wu, wd, wy_words, wy_scales, offs, out):
@@ -30,110 +40,107 @@ def tile_list_hot_neurons_kernel(tc, xt_words, xt_scales, wu, wd, wy_words, wy_s
 
         offsets = keep.tile([P, J // 16], U16, name="offsets")
         wu_rows = [keep.tile([P, R], F32, name="wu%d" % i) for i in range(PACK)]
-        wd_rows = [placed.tile([P, R], F32, name="wd%d" % c, offset=c * 4 * R, align_bytes=64) for c in range(CHUNKS)]
+        wd_rows = [placed.tile([P, R], F32, name="wd%d" % c, offset=c * ROW_BYTES, align_bytes=64)
+                   for c in range(CHUNKS)]
         x_codes = keep.tile([P, T], I32, name="x_codes", align_bytes=64)
         y_codes = keep.tile([P, 2 * M], U8, name="y_codes", align_bytes=64)
-        x_plane = keep.tile([P, T], U8, name="x_plane", align_bytes=64)
-        y_plane = keep.tile([P, M], U8, name="y_plane", align_bytes=64)
+        x_scale = keep.tile([P, T], U8, name="x_scale", align_bytes=64)
+        y_scale = keep.tile([P, M], U8, name="y_scale", align_bytes=64)
         ident = keep.tile([P, P], F32, name="ident")
 
-        def load_plane(plane, scales):
-            for q in range(4):
-                nc.sync.dma_start(out=plane[32 * q:32 * q + 4, :].bitcast(I32),
+        def load_scales(tile, scales):
+            for q in range(QUADRANTS):
+                nc.sync.dma_start(out=tile[32 * q:32 * q + 4, :].bitcast(I32),
                                   in_=scales[0, 4 * q:4 * q + 4, :].bitcast(I32))
 
-        nc.gpsimd.memset(x_plane[:].bitcast(I32), 0)
-        nc.gpsimd.memset(y_plane[:].bitcast(I32), 0)
+        nc.gpsimd.memset(x_scale[:].bitcast(I32), 0)
+        nc.gpsimd.memset(y_scale[:].bitcast(I32), 0)
         make_identity(nc, ident[:])
-        wu_by_slot = wu.rearrange("(p i) r -> i p r", i=PACK)
-        nc.sync.dma_start(out=wu_rows[0][:], in_=wu_by_slot[0])
+
+        wu_by_value = wu.rearrange("(p i) r -> i p r", i=PACK)
+        nc.sync.dma_start(out=wu_rows[0][:], in_=wu_by_value[0])
         nc.sync.dma_start(offsets[:], offs)
-        load_plane(x_plane, xt_scales)
+        load_scales(x_scale, xt_scales)
         for i in range(1, PACK):
-            nc.sync.dma_start(out=wu_rows[i][:], in_=wu_by_slot[i])
+            nc.sync.dma_start(out=wu_rows[i][:], in_=wu_by_value[i])
         nc.sync.dma_start(out=x_codes[:], in_=xt_words[0].rearrange("p n t -> p (n t)").bitcast(I32))
-        load_plane(y_plane, wy_scales)
+        load_scales(y_scale, wy_scales)
         nc.sync.dma_start(out=y_codes[:].bitcast(I32), in_=wy_words[0].bitcast(I32))
         for c in range(CHUNKS):
             nc.sync.dma_start(out=wd_rows[c][:], in_=wd[c * P:(c + 1) * P, :])
 
-        wu_bf = keep.tile([P, PACK * J], BF16, name="wu_bf", tag="wu_bf", align_bytes=64)
-        wu_view = wu_bf[:].rearrange("p (u e g r i) -> p i g u r e", u=2, e=2, g=16, r=8, i=PACK)
+        wu_bf = keep.tile([P, PACK * J], BF16, name="wu_bf", align_bytes=64)
+        wu_view = wu_bf[:].rearrange("p (u e g r i) -> p i g u r e", u=2, e=2, g=BLOCKS, r=8, i=PACK)
         for i in range(PACK):
             nc.vector.tensor_copy(out=wu_view[:, i], in_=wu_rows[i][:].indirect(offsets[:]))
         u_codes = keep.tile([P, J], U32, name="u_codes", align_bytes=64)
-        u_plane = keep.tile([P, J], U8, name="u_plane", align_bytes=64)
-        nc.vector.quantize_mx(out=u_codes[:].bitcast(FP8X4), scales=u_plane[:], in_=wu_bf[:])
+        u_scale = keep.tile([P, J], U8, name="u_scale", align_bytes=64)
+        nc.vector.quantize_mx(out=u_codes[:].bitcast(FP8X4), scales=u_scale[:], in_=wu_bf[:])
 
-        h_codes = [placed.tile([P, T // 2], U32, name="h_codes%d" % h, offset=h * 4 * R, align_bytes=64) for h in range(2)]
-        h_plane = [keep.tile([P, T // 2], U8, name="h_plane%d" % h, align_bytes=64) for h in range(2)]
-        h_bf = [keep.tile([P, PACK * T // 2], BF16, name="h_bf%d" % h, tag="h_bf%d" % h, align_bytes=64)
-                for h in range(2)]
-        for b in range(4):
-            toks = slice(b * P, (b + 1) * P)
-            acc = psum.tile([P, PACK, P], F32, name="acc%d" % b, tag="acc%d" % b)
+        h_codes = [placed.tile([P, HALF], U32, name="h_codes%d" % h, offset=h * ROW_BYTES, align_bytes=64)
+                   for h in range(2)]
+        h_scale = [keep.tile([P, HALF], U8, name="h_scale%d" % h, align_bytes=64) for h in range(2)]
+        h_bf = [keep.tile([P, PACK * HALF], BF16, name="h_bf%d" % h, align_bytes=64) for h in range(2)]
+        for b in range(QUARTERS):
+            h = b // 2
+            tokens = slice(b * P, (b + 1) * P)
+            pre = psum.tile([P, PACK, P], F32, name="acc%d" % b)
             for s in range(PACK):
                 cols = slice(s * P, (s + 1) * P)
-                nc.tensor.matmul_mx(out=acc[:, s, :], lhsT=u_codes[:, cols].bitcast(FP8X4), lhsT_scale=u_plane[:, cols],
-                                    rhs=x_codes[:, toks].bitcast(FP8X4), rhs_scale=x_plane[:, toks],
+                nc.tensor.matmul_mx(out=pre[:, s, :], lhsT=u_codes[:, cols].bitcast(FP8X4), lhsT_scale=u_scale[:, cols],
+                                    rhs=x_codes[:, tokens].bitcast(FP8X4), rhs_scale=x_scale[:, tokens],
                                     start=True, stop=True)
-            dst = h_bf[b // 2][:, (b % 2) * PACK * P:(b % 2 + 1) * PACK * P].rearrange("p (t s) -> p t s", s=PACK)
-            nc.scalar.activation(out=dst, in_=acc[:].rearrange("p s t -> p t s"), func=RELU)
+            grouped = h_bf[h][:, (b % 2) * PACK * P:(b % 2 + 1) * PACK * P].rearrange("p (t s) -> p t s", s=PACK)
+            nc.scalar.activation(out=grouped, in_=pre[:].rearrange("p s t -> p t s"), func=RELU)
             if b % 2 == 1:
-                nc.vector.quantize_mx(out=h_codes[b // 2][:].bitcast(FP8X4), scales=h_plane[b // 2][:], in_=h_bf[b // 2][:])
+                nc.vector.quantize_mx(out=h_codes[h][:].bitcast(FP8X4), scales=h_scale[h][:], in_=h_bf[h][:])
 
         for c in range(CHUNKS):
             picked = keep.tile([P, J], BF16, name="picked%d" % c, align_bytes=64)
-            nc.vector.tensor_copy(out=picked[:].rearrange("p (u g i) -> p g u i", u=2, g=16),
+            nc.vector.tensor_copy(out=picked[:].rearrange("p (u g n) -> p g u n", u=2, g=BLOCKS),
                                   in_=wd_rows[c][:].indirect(offsets[:]))
-            words = picked[:].bitcast(F32)
-            turned = psum.tile([P, 2, P], F32, name="turned%d" % c, tag=("acc0", "acc3", "turned2", "turned3")[c])
+            pairs = picked[:].bitcast(F32)
+            turned = psum.tile([P, 2, P], F32, name="turned%d" % c, tag=TURN_BANK[c])
             for u in range(2):
-                nc.tensor.transpose(turned[:, u, :], words[:, u * P:(u + 1) * P], ident[:])
-            d_bf = keep.tile([P, PACK * P], BF16, name="d_bf%d" % c,
-                             tag="d_bf%d" % c, align_bytes=64)
+                nc.tensor.transpose(turned[:, u, :], pairs[:, u * P:(u + 1) * P], ident[:])
+            d_bf = keep.tile([P, PACK * P], BF16, name="d_bf%d" % c, align_bytes=64)
             nc.scalar.copy(out=d_bf[:].bitcast(F32).rearrange("p (m u) -> p m u", u=2),
                            in_=turned[:].rearrange("p u m -> p m u"))
-            if c < CHUNKS - 1:
-                d_codes = placed.tile([P, P], U32, name="d_codes%d" % c, offset=(c + 1) * 4 * R + 2 * T, align_bytes=64)
+            if c < LAST:
+                d_codes = placed.tile([P, P], U32, name="d_codes%d" % c,
+                                      offset=(2 + c // 2) * ROW_BYTES + c * CODE_BYTES, align_bytes=64)
             else:
                 d_codes = keep.tile([P, P], U32, name="d_codes%d" % c, align_bytes=64)
-            d_plane = keep.tile([P, P], U8, name="d_plane%d" % c, align_bytes=64)
-            nc.vector.quantize_mx(out=d_codes[:].bitcast(FP8X4), scales=d_plane[:], in_=d_bf[:])
+            d_scale = keep.tile([P, P], U8, name="d_scale%d" % c, align_bytes=64)
+            nc.vector.quantize_mx(out=d_codes[:].bitcast(FP8X4), scales=d_scale[:], in_=d_bf[:])
 
-            y_w = y_codes[:, 2 * c * P:2 * (c + 1) * P].bitcast(FP4X4)
-            y_s = y_plane[:, c * P:(c + 1) * P]
-            res = keep.tile([P, T], F32, name="res%d" % c)
+            y_cols = y_codes[:, 2 * c * P:2 * (c + 1) * P].bitcast(FP4X4)
+            y_cols_scale = y_scale[:, c * P:(c + 1) * P]
+            result = keep.tile([P, T], F32, name="result%d" % c)
             rows = slice(c * P, (c + 1) * P)
-            if c < CHUNKS - 1:
-                acc = psum.tile([P, T], F32, name="total%d" % c, tag=("acc0", "acc3", "turned2")[c])
-                if c == CHUNKS - 2:
-                    nc.tensor.matmul_mx(out=acc[:], lhsT=y_w, lhsT_scale=y_s,
-                                        rhs=x_codes[:].bitcast(FP8X4), rhs_scale=x_plane[:], start=True, stop=True)
-                nc.tensor.matmul_mx(out=acc[:], lhsT=y_w, lhsT_scale=y_s,
-                                    rhs=x_codes[:].bitcast(FP8X4), rhs_scale=x_plane[:], start=True, stop=False)
+            if c < LAST:
+                total = psum.tile([P, T], F32, name="total%d" % c, tag=TURN_BANK[c])
+                nc.tensor.matmul_mx(out=total[:], lhsT=y_cols, lhsT_scale=y_cols_scale,
+                                    rhs=x_codes[:].bitcast(FP8X4), rhs_scale=x_scale[:], start=True, stop=False)
                 for h in range(2):
-                    nc.tensor.matmul_mx(out=acc[:, h * (T // 2):(h + 1) * (T // 2)],
-                                        lhsT=d_codes[:].bitcast(FP8X4), lhsT_scale=d_plane[:],
-                                        rhs=h_codes[h][:].bitcast(FP8X4), rhs_scale=h_plane[h][:],
+                    nc.tensor.matmul_mx(out=total[:, h * HALF:(h + 1) * HALF],
+                                        lhsT=d_codes[:].bitcast(FP8X4), lhsT_scale=d_scale[:],
+                                        rhs=h_codes[h][:].bitcast(FP8X4), rhs_scale=h_scale[h][:],
                                         start=False, stop=(h == 1))
-                nc.scalar.copy(out=res[:], in_=acc[:])
-                nc.sync.dma_start(out=out[rows, :], in_=res[:])
+                nc.scalar.copy(out=result[:], in_=total[:])
+                nc.sync.dma_start(out=out[rows, :], in_=result[:])
             else:
-                accs = [psum.tile([P, T // 2], F32, name="last%d" % h, tag=("acc0", "acc3")[h]) for h in range(2)]
-                for b in range(4):
-                    toks = slice(b * P, (b + 1) * P)
+                halves = [psum.tile([P, HALF], F32, name="last%d" % h, tag=LAST_BANK[h]) for h in range(2)]
+                for b in range(QUARTERS):
+                    tokens = slice(b * P, (b + 1) * P)
                     part = slice((b % 2) * P, (b % 2 + 1) * P)
-                    nc.tensor.matmul_mx(out=accs[b // 2][:, part], lhsT=y_w, lhsT_scale=y_s,
-                                        rhs=x_codes[:, toks].bitcast(FP8X4), rhs_scale=x_plane[:, toks],
+                    nc.tensor.matmul_mx(out=halves[b // 2][:, part], lhsT=y_cols, lhsT_scale=y_cols_scale,
+                                        rhs=x_codes[:, tokens].bitcast(FP8X4), rhs_scale=x_scale[:, tokens],
                                         start=(b % 2 == 0), stop=False)
-                for h in range(2):
-                    half = slice(h * (T // 2), (h + 1) * (T // 2))
-                    nc.tensor.matmul_mx(out=accs[h][:], lhsT=d_codes[:].bitcast(FP8X4), lhsT_scale=d_plane[:],
-                                        rhs=h_codes[h][:].bitcast(FP8X4), rhs_scale=h_plane[h][:],
+                for h, copy_out in enumerate((nc.vector.tensor_copy, nc.scalar.copy)):
+                    tokens = slice(h * HALF, (h + 1) * HALF)
+                    nc.tensor.matmul_mx(out=halves[h][:], lhsT=d_codes[:].bitcast(FP8X4), lhsT_scale=d_scale[:],
+                                        rhs=h_codes[h][:].bitcast(FP8X4), rhs_scale=h_scale[h][:],
                                         start=False, stop=True)
-                    if h == 0:
-                        nc.vector.tensor_copy(out=res[:, half], in_=accs[h][:])
-                    else:
-                        nc.scalar.copy(out=res[:, half], in_=accs[h][:])
-                    nc.sync.dma_start(out=out[rows, half], in_=res[:, half])
+                    copy_out(out=result[:, tokens], in_=halves[h][:])
+                    nc.sync.dma_start(out=out[rows, tokens], in_=result[:, tokens])

from contextlib import ExitStack

import concourse.mybir as mybir
from concourse.masks import make_identity

K, T, R, J, M = 512, 512, 2048, 512, 512
FLOPS = 2 * T * (K * J + J * M + K * M)

F32 = mybir.dt.float32
BF16 = mybir.dt.bfloat16
I32 = mybir.dt.int32
U32 = mybir.dt.uint32
U16 = mybir.dt.uint16
U8 = mybir.dt.uint8
FP8X4 = mybir.dt.float8_e4m3fn_x4
FP4X4 = mybir.dt.float4_e2m1fn_x4
RELU = mybir.ActivationFunctionType.Relu

P = 128
PACK = 4
BLOCKS = J // 32
QUADRANTS = 4
CHUNKS = M // P
LAST = CHUNKS - 1
QUARTERS = T // P
HALF = T // 2
ROW_BYTES = 4 * R
CODE_BYTES = 4 * P

TURN_BANK = ("acc0", "acc3", "turn2", "turn3")
LAST_BANK = ("acc1", "acc2")


def tile_list_hot_neurons_kernel(tc, xt_words, xt_scales, wu, wd, wy_words, wy_scales, offs, out):
    nc = tc.nc
    with ExitStack() as ctx:
        keep = ctx.enter_context(tc.tile_pool(name="keep", bufs=1))
        placed = ctx.enter_context(tc.tile_pool(name="placed", bufs=1))
        psum = ctx.enter_context(tc.psum_pool(name="psum", bufs=1))

        offsets = keep.tile([P, J // 16], U16, name="offsets")
        wu_rows = [keep.tile([P, R], F32, name="wu%d" % i) for i in range(PACK)]
        wd_rows = [placed.tile([P, R], F32, name="wd%d" % c, offset=c * ROW_BYTES, align_bytes=64)
                   for c in range(CHUNKS)]
        x_codes = keep.tile([P, T], I32, name="x_codes", align_bytes=64)
        y_codes = keep.tile([P, 2 * M], U8, name="y_codes", align_bytes=64)
        x_scale = keep.tile([P, T], U8, name="x_scale", align_bytes=64)
        y_scale = keep.tile([P, M], U8, name="y_scale", align_bytes=64)
        ident = keep.tile([P, P], F32, name="ident")

        def load_scales(tile, scales):
            for q in range(QUADRANTS):
                nc.sync.dma_start(out=tile[32 * q:32 * q + 4, :].bitcast(I32),
                                  in_=scales[0, 4 * q:4 * q + 4, :].bitcast(I32))

        nc.gpsimd.memset(x_scale[:].bitcast(I32), 0)
        nc.gpsimd.memset(y_scale[:].bitcast(I32), 0)
        make_identity(nc, ident[:])

        wu_by_value = wu.rearrange("(p i) r -> i p r", i=PACK)
        nc.sync.dma_start(out=wu_rows[0][:], in_=wu_by_value[0])
        nc.sync.dma_start(offsets[:], offs)
        load_scales(x_scale, xt_scales)
        for i in range(1, PACK):
            nc.sync.dma_start(out=wu_rows[i][:], in_=wu_by_value[i])
        nc.sync.dma_start(out=x_codes[:], in_=xt_words[0].rearrange("p n t -> p (n t)").bitcast(I32))
        load_scales(y_scale, wy_scales)
        nc.sync.dma_start(out=y_codes[:].bitcast(I32), in_=wy_words[0].bitcast(I32))
        for c in range(CHUNKS):
            nc.sync.dma_start(out=wd_rows[c][:], in_=wd[c * P:(c + 1) * P, :])

        wu_bf = keep.tile([P, PACK * J], BF16, name="wu_bf", align_bytes=64)
        wu_view = wu_bf[:].rearrange("p (u e g r i) -> p i g u r e", u=2, e=2, g=BLOCKS, r=8, i=PACK)
        for i in range(PACK):
            nc.vector.tensor_copy(out=wu_view[:, i], in_=wu_rows[i][:].indirect(offsets[:]))
        u_codes = keep.tile([P, J], U32, name="u_codes", align_bytes=64)
        u_scale = keep.tile([P, J], U8, name="u_scale", align_bytes=64)
        nc.vector.quantize_mx(out=u_codes[:].bitcast(FP8X4), scales=u_scale[:], in_=wu_bf[:])

        h_codes = [placed.tile([P, HALF], U32, name="h_codes%d" % h, offset=h * ROW_BYTES, align_bytes=64)
                   for h in range(2)]
        h_scale = [keep.tile([P, HALF], U8, name="h_scale%d" % h, align_bytes=64) for h in range(2)]
        h_bf = [keep.tile([P, PACK * HALF], BF16, name="h_bf%d" % h, align_bytes=64) for h in range(2)]
        for b in range(QUARTERS):
            h = b // 2
            tokens = slice(b * P, (b + 1) * P)
            pre = psum.tile([P, PACK, P], F32, name="acc%d" % b)
            for s in range(PACK):
                cols = slice(s * P, (s + 1) * P)
                nc.tensor.matmul_mx(out=pre[:, s, :], lhsT=u_codes[:, cols].bitcast(FP8X4), lhsT_scale=u_scale[:, cols],
                                    rhs=x_codes[:, tokens].bitcast(FP8X4), rhs_scale=x_scale[:, tokens],
                                    start=True, stop=True)
            grouped = h_bf[h][:, (b % 2) * PACK * P:(b % 2 + 1) * PACK * P].rearrange("p (t s) -> p t s", s=PACK)
            nc.scalar.activation(out=grouped, in_=pre[:].rearrange("p s t -> p t s"), func=RELU)
            if b % 2 == 1:
                nc.vector.quantize_mx(out=h_codes[h][:].bitcast(FP8X4), scales=h_scale[h][:], in_=h_bf[h][:])

        for c in range(CHUNKS):
            picked = keep.tile([P, J], BF16, name="picked%d" % c, align_bytes=64)
            nc.vector.tensor_copy(out=picked[:].rearrange("p (u g n) -> p g u n", u=2, g=BLOCKS),
                                  in_=wd_rows[c][:].indirect(offsets[:]))
            pairs = picked[:].bitcast(F32)
            turned = psum.tile([P, 2, P], F32, name="turned%d" % c, tag=TURN_BANK[c])
            for u in range(2):
                nc.tensor.transpose(turned[:, u, :], pairs[:, u * P:(u + 1) * P], ident[:])
            d_bf = keep.tile([P, PACK * P], BF16, name="d_bf%d" % c, align_bytes=64)
            nc.scalar.copy(out=d_bf[:].bitcast(F32).rearrange("p (m u) -> p m u", u=2),
                           in_=turned[:].rearrange("p u m -> p m u"))
            if c < LAST:
                d_codes = placed.tile([P, P], U32, name="d_codes%d" % c,
                                      offset=(2 + c // 2) * ROW_BYTES + c * CODE_BYTES, align_bytes=64)
            else:
                d_codes = keep.tile([P, P], U32, name="d_codes%d" % c, align_bytes=64)
            d_scale = keep.tile([P, P], U8, name="d_scale%d" % c, align_bytes=64)
            nc.vector.quantize_mx(out=d_codes[:].bitcast(FP8X4), scales=d_scale[:], in_=d_bf[:])

            y_cols = y_codes[:, 2 * c * P:2 * (c + 1) * P].bitcast(FP4X4)
            y_cols_scale = y_scale[:, c * P:(c + 1) * P]
            result = keep.tile([P, T], F32, name="result%d" % c)
            rows = slice(c * P, (c + 1) * P)
            if c < LAST:
                total = psum.tile([P, T], F32, name="total%d" % c, tag=TURN_BANK[c])
                nc.tensor.matmul_mx(out=total[:], lhsT=y_cols, lhsT_scale=y_cols_scale,
                                    rhs=x_codes[:].bitcast(FP8X4), rhs_scale=x_scale[:], start=True, stop=False)
                for h in range(2):
                    nc.tensor.matmul_mx(out=total[:, h * HALF:(h + 1) * HALF],
                                        lhsT=d_codes[:].bitcast(FP8X4), lhsT_scale=d_scale[:],
                                        rhs=h_codes[h][:].bitcast(FP8X4), rhs_scale=h_scale[h][:],
                                        start=False, stop=(h == 1))
                nc.scalar.copy(out=result[:], in_=total[:])
                nc.sync.dma_start(out=out[rows, :], in_=result[:])
            else:
                halves = [psum.tile([P, HALF], F32, name="last%d" % h, tag=LAST_BANK[h]) for h in range(2)]
                for b in range(QUARTERS):
                    tokens = slice(b * P, (b + 1) * P)
                    part = slice((b % 2) * P, (b % 2 + 1) * P)
                    nc.tensor.matmul_mx(out=halves[b // 2][:, part], lhsT=y_cols, lhsT_scale=y_cols_scale,
                                        rhs=x_codes[:, tokens].bitcast(FP8X4), rhs_scale=x_scale[:, tokens],
                                        start=(b % 2 == 0), stop=False)
                for h, copy_out in enumerate((nc.vector.tensor_copy, nc.scalar.copy)):
                    tokens = slice(h * HALF, (h + 1) * HALF)
                    nc.tensor.matmul_mx(out=halves[h][:], lhsT=d_codes[:].bitcast(FP8X4), lhsT_scale=d_scale[:],
                                        rhs=h_codes[h][:].bitcast(FP8X4), rhs_scale=h_scale[h][:],
                                        start=False, stop=True)
                    copy_out(out=result[:, tokens], in_=halves[h][:])
                    nc.sync.dma_start(out=out[rows, tokens], in_=result[:, tokens])
